import numpy as np
import ml_dtypes


def mxq(x, axis, fmt="e4m3"):
    dtype, down = {"e4m3": (ml_dtypes.float8_e4m3fn, 7), "e5m2": (ml_dtypes.float8_e5m2, 14)}[fmt]
    v = np.moveaxis(np.asarray(x, np.float32).astype(ml_dtypes.bfloat16).astype(np.float64), axis, -1)
    blocks = v.reshape(v.shape[:-1] + (-1, 32))
    amax = np.abs(blocks).max(-1, keepdims=True)
    byte = np.maximum(np.where(amax > 0, np.frexp(amax)[1] - 1 + 127, 0) - down, 1)
    scale = np.exp2(byte - 127.0)
    codes = (blocks / scale).astype(np.float32).astype(dtype).astype(np.float64)
    return np.moveaxis((codes * scale).reshape(v.shape), -1, axis)


WIDE = False


def mx_kscale(k):
    if not WIDE:
        return np.ones(k)
    levels = np.array([10, -10, 5, -5, 0])
    if k % 512:
        return np.exp2(np.random.permutation(np.resize(levels, k // 32))).repeat(32)
    a = np.empty((k // 512, 16))
    for p in range(k // 512):
        a[p, :8] = np.random.permutation(np.resize(levels, 8))
        for g in range(8):
            far = levels[np.abs(levels - a[p, g]) >= 10]
            a[p, g + 8] = far[np.random.randint(len(far))]
    return np.exp2(a.ravel()).repeat(32)


def f64(x):
    return np.asarray(x).astype(np.float64)


def striped(idx):
    return np.tile(np.asarray(idx).reshape(-1, 16).T, (8, 1)).astype(np.uint16)


def unstriped(offs):
    return offs[:16].T.reshape(-1).astype(np.int64)


E2M1 = np.array([0.0, 0.5, 1.0, 1.5, 2.0, 3.0, 4.0, 6.0, -0.0, -0.5, -1.0, -1.5, -2.0, -3.0, -4.0, -6.0])


def pack_weight(w, fmt):
    k, n = w.shape
    w = f64(np.asarray(w, np.float32).astype(ml_dtypes.bfloat16)).reshape(k // 32, 32, n)
    amax = np.abs(w).max(1)
    if fmt == "e4m3":
        byte = np.frexp(amax)[1] - 1 + 127 - 7
    else:
        mant, ex = np.frexp(amax / 6.0)
        byte = np.where(mant > 0.5, ex, ex - 1) + 127
    byte = np.clip(np.where(amax > 0, byte, 1), 1, 254)
    scaled = (w * np.exp2(127.0 - byte)[:, None, :]).reshape(k, n).astype(np.float32)
    by_word = np.ascontiguousarray(scaled.reshape(k // 512, 128, 4, n).transpose(0, 1, 3, 2))
    if fmt == "e4m3":
        words = by_word.astype(ml_dtypes.float8_e4m3fn).view(np.uint8)
    else:
        c = by_word.astype(ml_dtypes.float4_e2m1fn).view(np.uint8) & 0xF
        words = (c[..., 0::2] | (c[..., 1::2] << 4)).reshape(k // 512, 128, 2 * n)
    return np.ascontiguousarray(words), np.ascontiguousarray(byte.astype(np.uint8).reshape(k // 512, 16, n))


def unpack_weight(words, scales, fmt):
    g, _, n = scales.shape
    words = np.ascontiguousarray(words).reshape(g, 128, n, -1)
    if fmt == "e4m3":
        vals = words.view(ml_dtypes.float8_e4m3fn).astype(np.float64)
    else:
        nib = np.empty((g, 128, n, 4), np.uint8)
        nib[..., 0::2] = words & 0xF
        nib[..., 1::2] = words >> 4
        vals = E2M1[nib]
    vals = vals * np.repeat(np.exp2(scales.astype(np.float64) - 127.0), 8, axis=1)[..., None]
    return vals.transpose(0, 1, 3, 2).reshape(g * 512, n)


D, T, I, Q, E, U, M = 512, 2048, 512, 256, 512, 1024, 1024


def setup_inputs():
    n = np.random.standard_normal
    idx = np.random.permutation(T)[:I]
    idx2 = np.random.permutation(U)[:I]
    idx3 = np.random.permutation(M)[:Q]
    fd = mx_kscale(D)
    fi = mx_kscale(I)
    ti = np.ones(T)
    ti[idx] = fi
    keysp = pack_weight(n((D, T)) / fd[:, None], "e2m1")
    return {
        "query": (n((D, Q)) * 0.9 / np.sqrt(D) * fd[:, None]).astype(np.float32),
        "keys_words": keysp[0],
        "keys_scales": keysp[1],
        "query2": (n((D, Q)) * 0.9 / np.sqrt(D) * fd[:, None]).astype(np.float32),
        "notes": (n((D, U)) / fd[:, None]).astype(np.float32),
        "lam": (np.random.uniform(0.1, 0.5, (Q, 1))).astype(np.float32),
        "os": (np.random.uniform(0.02, 0.08, (1, I)) * fi).astype(np.float32),
        "vals": (n((E, T)) / ti).astype(np.float32),
        "old": (n((E, M)) * 2.0).astype(np.float32),
        "fade": (np.random.uniform(0.3, 0.9, (1, M))).astype(np.float32),
        "offs": striped(idx),
        "offs2": striped(idx2),
        "offs3": striped(idx3),
    }


def reference(query, keys_words, keys_scales, query2, notes, lam, os, vals, old, fade, offs, offs2, offs3):
    idx = unstriped(offs)
    idx2 = unstriped(offs2)
    idx3 = unstriped(offs3)
    keysu = unpack_weight(keys_words, keys_scales, "e2m1")
    queryq = mxq(f64(query), 0, "e4m3")
    keysidxg = keysu[:, idx]
    a = queryq.T @ keysidxg
    query2q = mxq(f64(query2), 0, "e4m3")
    notesidx2q = mxq(f64(notes)[:, idx2], 0, "e4m3")
    b = query2q.T @ notesidx2q
    s = np.maximum(a, b) + np.minimum(a, b) * f64(lam)
    w = np.maximum(s, 0.0)
    wo1 = w * f64(os)
    wt1 = wo1.T
    vt1 = f64(vals)[:, idx].T
    vt1q = mxq(vt1, 0, "e4m3")
    wt1q = mxq(wt1, 0, "e4m3")
    o = vt1q.T @ wt1q
    of = np.zeros((E, M))
    of[:, idx3] = o
    y = f64(old) * f64(fade) + of
    return y

@@ -1,0 +1,245 @@
+from contextlib import ExitStack
+
+import concourse.mybir as mybir
+from concourse.masks import make_identity
+
+D, T, I, Q, E, U, M = 512, 2048, 512, 256, 512, 1024, 1024
+FLOPS = 2 * Q * I * D * 2 + 2 * E * Q * I
+
+F32 = mybir.dt.float32
+BF16 = mybir.dt.bfloat16
+I32 = mybir.dt.int32
+U32 = mybir.dt.uint32
+U16 = mybir.dt.uint16
+U8 = mybir.dt.uint8
+FP8X4 = mybir.dt.float8_e4m3fn_x4
+FP4X4 = mybir.dt.float4_e2m1fn_x4
+ALU = mybir.AluOpType
+COPY = mybir.ActivationFunctionType.Copy
+
+P = 128
+PACK = 4
+BANK = 512
+
+
+def tile_attend_twopools_written_lean_kernel(
+    tc, query, keys_words, keys_scales, query2, notes, lam, slot_factor, vals, old, fade, offs, offs2, offs3, out
+):
+    nc = tc.nc
+    halves = Q // P
+    blocks = E // P
+    with ExitStack() as ctx:
+        sb = ctx.enter_context(tc.tile_pool(name="sb", bufs=1))
+        ps = ctx.enter_context(tc.psum_pool(name="ps", bufs=1))
+
+        def buf(name, shape, dtype, on=None):
+            return sb.tile(shape, dtype, name=name, tag=on or name, align_bytes=64)
+
+        slot_token = buf("slot_token", [P, I // 16], U16)
+        slot_note = buf("slot_note", [P, I // 16], U16)
+        row_place = buf("row_place", [P, Q // 16], U16)
+        key_words = buf("key_words", [P, T], U16)
+        key_scales = buf("key_scales", [P, T], U8)
+        note_planes = [buf("note_plane%d" % t, [P, U], F32) for t in range(PACK)]
+        q_raw = [buf("q_raw%d" % n, [P, PACK, Q], F32) for n in range(2)]
+        val_rows = [buf("val_rows%d" % j, [P, T], F32) for j in range(blocks)]
+        old_rows = [buf("old_rows%d" % j, [P, M], F32) for j in range(blocks)]
+        placed = [buf("placed%d" % j, [P, M], F32) for j in range(2)]
+        rows = buf("rows", [P, P], F32)
+        factor_col = buf("factor_col", [P, PACK], F32)
+        ident = buf("ident", [P, P], F32)
+
+        nc.vector.memset(key_scales[:].bitcast(I32), 0)
+        nc.vector.memset(rows[:], 0.0)
+        for w in placed:
+            nc.vector.memset(w[:], 0.0)
+        make_identity(nc, ident[:])
+
+        notes_by_plane = notes.rearrange("(p t) u -> t p u", t=PACK)
+        nc.sync.dma_start(slot_note[:], offs2)
+        nc.sync.dma_start(note_planes[0][:], notes_by_plane[0])
+        for quad in range(4):
+            nc.sync.dma_start(
+                key_scales[32 * quad : 32 * quad + 4, :].bitcast(I32),
+                keys_scales[0, 4 * quad : 4 * quad + 4, :].bitcast(I32),
+            )
+        nc.sync.dma_start(slot_token[:], offs)
+        nc.sync.dma_start(key_words[:].bitcast(I32), keys_words[0].bitcast(I32))
+        nc.sync.dma_start(note_planes[1][:], notes_by_plane[1])
+        nc.sync.dma_start(rows[0:8, :], fade.rearrange("o (r n) -> (o r) n", n=P))
+        nc.sync.dma_start(rows[8:10, :], lam.rearrange("(r n) o -> r (n o)", n=P))
+        nc.sync.dma_start(note_planes[2][:], notes_by_plane[2])
+        nc.sync.dma_start(note_planes[3][:], notes_by_plane[3])
+        nc.sync.dma_start(q_raw[1][:], query2.rearrange("(p t) q -> p t q", t=PACK))
+        nc.sync.dma_start(q_raw[0][:], query.rearrange("(p t) q -> p t q", t=PACK))
+        nc.sync.dma_start(val_rows[0][:], vals[0:P, :])
+        nc.sync.dma_start(factor_col[:], slot_factor.rearrange("o (p t) -> p (o t)", t=PACK))
+        nc.sync.dma_start(val_rows[1][:], vals[P : 2 * P, :])
+        nc.sync.dma_start(row_place[:], offs3)
+        nc.sync.dma_start(val_rows[2][:], vals[2 * P : 3 * P, :])
+        nc.sync.dma_start(old_rows[0][:], old[0:P, :])
+        nc.sync.dma_start(old_rows[1][:], old[P : 2 * P, :])
+        nc.sync.dma_start(val_rows[3][:], vals[3 * P : 4 * P, :])
+        nc.sync.dma_start(old_rows[2][:], old[2 * P : 3 * P, :])
+        nc.sync.dma_start(old_rows[3][:], old[3 * P : 4 * P, :])
+
+        note_picked = buf("note_picked", [P, PACK, I], BF16)
+        key_words_picked = buf("key_words_picked", [P, I], U16)
+        key_scales_picked = buf("key_scales_picked", [P, I], U8)
+        nc.vector.tensor_copy(key_words_picked[:], key_words[:].indirect(slot_token[:]))
+        nc.vector.tensor_copy(key_scales_picked[:], key_scales[:].indirect(slot_token[:]))
+        for t in range(PACK - 1):
+            nc.scalar.activation(note_picked[:, t, :], note_planes[t][:].indirect(slot_note[:]), COPY)
+        last = PACK - 1
+        nc.scalar.activation(note_picked[:, last, : I // 2], note_planes[last][:].indirect(slot_note[:, : I // 32]), COPY)
+        nc.vector.tensor_copy(note_picked[:, last, I // 2 :], note_planes[last][:].indirect(slot_note[:, I // 32 :]))
+
+        rows_turned = ps.tile([P, P], F32, name="rows_turned", tag="bank_v0")
+        nc.tensor.transpose(rows_turned[:], rows[:], ident[:])
+        columns = buf("columns", [P, 16], F32, on="note_plane1")
+        nc.scalar.copy(columns[:], rows_turned[:, 0:16])
+        fade_bank = [ps.tile([P, BANK], F32, name="fade_bank%d" % h) for h in range(M // BANK)]
+        for r in range(M // P):
+            h, c = divmod(r, BANK // P)
+            nc.tensor.transpose(fade_bank[h][:, c * P : (c + 1) * P], columns[:, r : r + 1].to_broadcast([P, P]), ident[:])
+
+        note_bf = buf("note_bf", [P, I * PACK], BF16)
+        note_codes = buf("note_codes", [P, I], U32)
+        note_scales = buf("note_scales", [P, I], U8)
+        q_bf = [buf("q_bf%d" % n, [P, Q * PACK], BF16) for n in range(2)]
+        q_codes = [buf("q_codes%d" % n, [P, Q], U32) for n in range(2)]
+        q_scales = [buf("q_scales%d" % n, [P, Q], U8) for n in range(2)]
+
+        nc.vector.tensor_copy(
+            note_bf[:].rearrange("p (c i t) -> p c t i", i=4, t=PACK),
+            note_picked[:].rearrange("p t (c i) -> p c t i", i=4),
+        )
+        for n in (1, 0):
+            nc.scalar.copy(
+                q_bf[n][:].rearrange("p (c i t) -> p c t i", i=4, t=PACK),
+                q_raw[n][:].rearrange("p t (c i) -> p c t i", i=4),
+            )
+        nc.vector.quantize_mx(note_codes[:].bitcast(FP8X4), note_scales[:], note_bf[:])
+        nc.vector.quantize_mx(q_codes[1][:].bitcast(FP8X4), q_scales[1][:], q_bf[1][:])
+        nc.vector.quantize_mx(q_codes[0][:].bitcast(FP8X4), q_scales[0][:], q_bf[0][:])
+
+        a_bank = [ps.tile([P, I], F32, name="a_bank%d" % h, tag="bank_a%d" % h) for h in range(halves)]
+        b_bank = [ps.tile([P, I], F32, name="b_bank%d" % h, tag="bank_b%d" % h) for h in range(halves)]
+        for h in range(halves):
+            cols = slice(h * P, (h + 1) * P)
+            nc.tensor.matmul_mx(
+                b_bank[h][:], lhsT=q_codes[1][:, cols].bitcast(FP8X4), lhsT_scale=q_scales[1][:, cols],
+                rhs=note_codes[:].bitcast(FP8X4), rhs_scale=note_scales[:], start=True, stop=True,
+            )
+        for h in range(halves):
+            cols = slice(h * P, (h + 1) * P)
+            nc.tensor.matmul_mx(
+                a_bank[h][:], lhsT=q_codes[0][:, cols].bitcast(FP8X4), lhsT_scale=q_scales[0][:, cols],
+                rhs=key_words_picked[:].bitcast(FP4X4), rhs_scale=key_scales_picked[:], start=True, stop=True,
+            )
+
+        val_codes = [buf("val_codes%d" % j, [P, P], U32) for j in range(blocks)]
+        val_scales = [buf("val_scales%d" % j, [P, P], U8) for j in range(blocks)]
+        val_picked = {}
+
+        def pick_values(j, into, by_scalar):
+            val_picked[j] = into
+            window = val_rows[j][:].indirect(slot_token[:])
+            if by_scalar:
+                nc.scalar.activation(into, window, COPY)
+            else:
+                nc.vector.tensor_copy(into, window)
+
+        def turn_values(j, bank, val_bf):
+            words = val_picked[j].bitcast(F32)
+            turned = ps.tile([P, 2, P], F32, name="val_turned%d" % j, tag=bank)
+            for u in range(2):
+                nc.tensor.transpose(turned[:, u, :], words[:, u : I // 2 : 2], ident[:])
+            nc.scalar.copy(
+                val_bf.rearrange("p (e u) -> p e u", u=2),
+                turned[:].rearrange("p u e -> p e u"),
+            )
+            nc.vector.quantize_mx(val_codes[j][:].bitcast(FP8X4), val_scales[j][:], val_bf.bitcast(BF16))
+
+        faded = [buf("faded%d" % n, [P, M], F32) for n in range(2)]
+        w_bf = faded[0][:, M // 4 : 3 * M // 4].bitcast(BF16)
+        b_flat = [buf("b_flat%d" % h, [P, I], F32) for h in range(halves)]
+        b_sb = [b_flat[h][:].rearrange("q (t s) -> q t s", t=PACK) for h in range(halves)]
+        larger = [buf("larger%d" % h, [P, PACK, P], F32) for h in range(halves)]
+        smaller = [buf("smaller%d" % h, [P, PACK, P], F32) for h in range(halves)]
+        smaller_lam = [buf("smaller_lam%d" % h, [P, PACK, P], F32) for h in range(halves)]
+        a_dealt = [a_bank[h][:].rearrange("q (s t) -> q t s", t=PACK) for h in range(halves)]
+        for h in range(halves):
+            nc.scalar.copy(b_sb[h], b_bank[h][:].rearrange("q (s t) -> q t s", t=PACK))
+        pick_values(0, q_bf[0][:, :I], True)
+        for h in range(halves):
+            nc.vector.tensor_tensor(smaller[h][:], a_dealt[h], b_sb[h], ALU.min)
+            nc.vector.tensor_tensor(larger[h][:], a_dealt[h], b_sb[h], ALU.max)
+            nc.vector.tensor_scalar(smaller_lam[h][:], smaller[h][:], columns[:, 8 + h : 9 + h], None, ALU.mult)
+        s_bank = [ps.tile([P, PACK, P], F32, name="s_bank%d" % h, tag="bank_b%d" % h) for h in range(halves)]
+        for h in range(halves):
+            for t in range(PACK):
+                nc.tensor.matmul(s_bank[h][:, t, :], larger[h][:, t, :], ident[:], start=(t == 0), stop=False, is_transpose=True)
+            for t in range(PACK):
+                nc.tensor.matmul(s_bank[h][:, t, :], smaller_lam[h][:, t, :], ident[:], start=False, stop=(t == PACK - 1), is_transpose=True)
+        turn_values(0, "bank_v0", faded[0][:, M // 2 : 3 * M // 4])
+        pick_values(1, b_flat[0][:, : I // 2].bitcast(BF16), True)
+        for h in range(halves):
+            nc.vector.scalar_tensor_tensor(
+                w_bf[:, h * BANK : (h + 1) * BANK].rearrange("p (q t) -> p q t", t=PACK),
+                s_bank[h][:].rearrange("p t q -> p q t"),
+                0.0,
+                factor_col[:].unsqueeze(1).to_broadcast([P, P, PACK]),
+                ALU.max,
+                ALU.mult,
+            )
+        w_codes = buf("w_codes", [P, Q], U32)
+        w_scales = buf("w_scales", [P, Q], U8)
+        nc.vector.quantize_mx(w_codes[:].bitcast(FP8X4), w_scales[:], w_bf)
+        pick_values(2, b_flat[1][:, : I // 2].bitcast(BF16), True)
+        turn_values(1, "bank_v1", buf("val_bf1", [P, Q], F32, on="val_rows2")[:])
+
+        o_sb = {}
+
+        def fade_old(j):
+            for h in range(M // BANK):
+                cols = slice(h * BANK, (h + 1) * BANK)
+                nc.vector.tensor_tensor(faded[min(j, 1)][:, cols], old_rows[j][:, cols], fade_bank[h][:], ALU.mult)
+
+        def sum_values(j, bank, into):
+            o_bank = ps.tile([P, Q], F32, name="o_bank%d" % j, tag=bank)
+            nc.tensor.matmul_mx(
+                o_bank[:], lhsT=val_codes[j][:].bitcast(FP8X4), lhsT_scale=val_scales[j][:],
+                rhs=w_codes[:].bitcast(FP8X4), rhs_scale=w_scales[:], start=True, stop=True,
+            )
+            o_sb[j] = into
+            nc.scalar.copy(into, o_bank[:])
+
+        def place(j):
+            nc.scalar.activation(placed[j % 2][:].indirect(row_place[:]), o_sb[j], COPY)
+
+        def finish(j, parts, total):
+            for part in range(parts):
+                cols = slice(part * M // parts, (part + 1) * M // parts)
+                nc.vector.tensor_tensor(total[:, cols], faded[min(j, 1)][:, cols], placed[j % 2][:, cols], ALU.add)
+                nc.sync.dma_start(out[j * P : (j + 1) * P, cols], total[:, cols])
+
+        turn_values(2, "bank_b1", faded[1][:, 3 * M // 8 : 5 * M // 8])
+        sum_values(0, "bank_a0", b_flat[1][:, :Q])
+        place(0)
+        fade_old(0)
+        sum_values(1, "bank_b1", buf("o_sb1", [P, Q], F32)[:])
+        place(1)
+        fade_old(1)
+        pick_values(3, buf("val_picked3", [P, I], BF16, on="old_rows1")[:], False)
+        finish(0, 1, buf("total0", [P, M], F32, on="val_rows3"))
+        sum_values(2, "bank_a1", buf("o_sb2", [P, Q], F32)[:])
+        finish(1, 1, faded[0])
+        turn_values(3, "bank_a0", buf("val_bf3", [P, Q], F32)[:])
+        place(2)
+        fade_old(2)
+        sum_values(3, "bank_b0", buf("o_sb3", [P, Q], F32)[:])
+        place(3)
+        finish(2, 1, buf("total2", [P, M], F32))
+        fade_old(3)
+        finish(3, 2, faded[1])

@@ -169,9 +169,9 @@ def tile_attend_twopools_written_lean_kernel(
         smaller = [buf("smaller%d" % h, [P, PACK, P], F32) for h in range(halves)]
         smaller_lam = [buf("smaller_lam%d" % h, [P, PACK, P], F32) for h in range(halves)]
         a_dealt = [a_bank[h][:].rearrange("q (s t) -> q t s", t=PACK) for h in range(halves)]
+        pick_values(0, buf("val_picked0", [P, I], BF16, on="q_raw0")[:], True)
         for h in range(halves):
             nc.scalar.copy(b_sb[h], b_bank[h][:].rearrange("q (s t) -> q t s", t=PACK))
-        pick_values(0, q_bf[0][:, :I], True)
         for h in range(halves):
             nc.vector.tensor_tensor(smaller[h][:], a_dealt[h], b_sb[h], ALU.min)
             nc.vector.tensor_tensor(larger[h][:], a_dealt[h], b_sb[h], ALU.max)
@@ -183,7 +183,7 @@ def tile_attend_twopools_written_lean_kernel(
             for t in range(PACK):
                 nc.tensor.matmul(s_bank[h][:, t, :], smaller_lam[h][:, t, :], ident[:], start=False, stop=(t == PACK - 1), is_transpose=True)
         turn_values(0, "bank_v0", faded[0][:, M // 2 : 3 * M // 4])
-        pick_values(1, b_flat[0][:, : I // 2].bitcast(BF16), True)
+        pick_values(1, buf("val_picked1", [P, I], BF16)[:], True)
         for h in range(halves):
             nc.vector.scalar_tensor_tensor(
                 w_bf[:, h * BANK : (h + 1) * BANK].rearrange("p (q t) -> p q t", t=PACK),
@@ -197,7 +197,7 @@ def tile_attend_twopools_written_lean_kernel(
         w_scales = buf("w_scales", [P, Q], U8)
         nc.vector.quantize_mx(w_codes[:].bitcast(FP8X4), w_scales[:], w_bf)
         pick_values(2, b_flat[1][:, : I // 2].bitcast(BF16), True)
-        turn_values(1, "bank_v1", buf("val_bf1", [P, Q], F32, on="val_rows2")[:])
+        turn_values(1, "bank_b0", buf("val_bf1", [P, Q], F32, on="val_rows2")[:])
 
         o_sb = {}
 

@@ -131,8 +131,6 @@ def tile_attend_twopools_written_lean_kernel(
                 b_bank[h][:], lhsT=q_codes[1][:, cols].bitcast(FP8X4), lhsT_scale=q_scales[1][:, cols],
                 rhs=note_codes[:].bitcast(FP8X4), rhs_scale=note_scales[:], start=True, stop=True,
             )
-        for h in range(halves):
-            cols = slice(h * P, (h + 1) * P)
             nc.tensor.matmul_mx(
                 a_bank[h][:], lhsT=q_codes[0][:, cols].bitcast(FP8X4), lhsT_scale=q_scales[0][:, cols],
                 rhs=key_words_picked[:].bitcast(FP4X4), rhs_scale=key_scales_picked[:], start=True, stop=True,
@@ -141,6 +139,7 @@ def tile_attend_twopools_written_lean_kernel(
         val_codes = [buf("val_codes%d" % j, [P, P], U32) for j in range(blocks)]
         val_scales = [buf("val_scales%d" % j, [P, P], U8) for j in range(blocks)]
         val_picked = {}
+        val_words = {}
 
         def pick_values(j, into, by_scalar):
             val_picked[j] = into
@@ -159,31 +158,37 @@ def tile_attend_twopools_written_lean_kernel(
                 val_bf.rearrange("p (e u) -> p e u", u=2),
                 turned[:].rearrange("p u e -> p e u"),
             )
-            nc.vector.quantize_mx(val_codes[j][:].bitcast(FP8X4), val_scales[j][:], val_bf.bitcast(BF16))
+            val_words[j] = val_bf
+
+        def quantise_values(j):
+            nc.vector.quantize_mx(val_codes[j][:].bitcast(FP8X4), val_scales[j][:], val_words[j].bitcast(BF16))
 
         faded = [buf("faded%d" % n, [P, M], F32) for n in range(2)]
         w_bf = faded[0][:, M // 4 : 3 * M // 4].bitcast(BF16)
         b_flat = [buf("b_flat%d" % h, [P, I], F32) for h in range(halves)]
         b_sb = [b_flat[h][:].rearrange("q (t s) -> q t s", t=PACK) for h in range(halves)]
         larger = [buf("larger%d" % h, [P, PACK, P], F32) for h in range(halves)]
-        smaller = [buf("smaller%d" % h, [P, PACK, P], F32) for h in range(halves)]
+        smaller_flat = [buf("smaller_flat%d" % h, [P, I], F32) for h in range(halves)]
+        smaller = [smaller_flat[h][:].rearrange("q (t s) -> q t s", t=PACK) for h in range(halves)]
         smaller_lam = [buf("smaller_lam%d" % h, [P, PACK, P], F32) for h in range(halves)]
         a_dealt = [a_bank[h][:].rearrange("q (s t) -> q t s", t=PACK) for h in range(halves)]
         pick_values(0, buf("val_picked0", [P, I], BF16, on="q_raw0")[:], True)
         for h in range(halves):
             nc.scalar.copy(b_sb[h], b_bank[h][:].rearrange("q (s t) -> q t s", t=PACK))
+        turn_values(0, "bank_v0", faded[0][:, M // 2 : 3 * M // 4])
+        quantise_values(0)
         for h in range(halves):
-            nc.vector.tensor_tensor(smaller[h][:], a_dealt[h], b_sb[h], ALU.min)
+            nc.vector.tensor_tensor(smaller[h], a_dealt[h], b_sb[h], ALU.min)
+            nc.scalar.activation(smaller_lam[h][:], smaller[h], COPY, scale=columns[:, 8 + h : 9 + h])
+        for h in range(halves):
             nc.vector.tensor_tensor(larger[h][:], a_dealt[h], b_sb[h], ALU.max)
-            nc.vector.tensor_scalar(smaller_lam[h][:], smaller[h][:], columns[:, 8 + h : 9 + h], None, ALU.mult)
         s_bank = [ps.tile([P, PACK, P], F32, name="s_bank%d" % h, tag="bank_b%d" % h) for h in range(halves)]
         for h in range(halves):
             for t in range(PACK):
-                nc.tensor.matmul(s_bank[h][:, t, :], larger[h][:, t, :], ident[:], start=(t == 0), stop=False, is_transpose=True)
+                nc.tensor.matmul(s_bank[h][:, t, :], smaller_lam[h][:, t, :], ident[:], start=(t == 0), stop=False, is_transpose=True)
             for t in range(PACK):
-                nc.tensor.matmul(s_bank[h][:, t, :], smaller_lam[h][:, t, :], ident[:], start=False, stop=(t == PACK - 1), is_transpose=True)
-        turn_values(0, "bank_v0", faded[0][:, M // 2 : 3 * M // 4])
-        pick_values(1, buf("val_picked1", [P, I], BF16)[:], True)
+                nc.tensor.matmul(s_bank[h][:, t, :], larger[h][:, t, :], ident[:], start=False, stop=(t == PACK - 1), is_transpose=True)
+        pick_values(1, smaller_flat[0][:, : I // 2].bitcast(BF16), True)
         for h in range(halves):
             nc.vector.scalar_tensor_tensor(
                 w_bf[:, h * BANK : (h + 1) * BANK].rearrange("p (q t) -> p q t", t=PACK),
@@ -195,9 +200,12 @@ def tile_attend_twopools_written_lean_kernel(
             )
         w_codes = buf("w_codes", [P, Q], U32)
         w_scales = buf("w_scales", [P, Q], U8)
-        nc.vector.quantize_mx(w_codes[:].bitcast(FP8X4), w_scales[:], w_bf)
+        for h in range(halves):
+            cols = slice(h * P, (h + 1) * P)
+            nc.vector.quantize_mx(w_codes[:, cols].bitcast(FP8X4), w_scales[:, cols], w_bf[:, h * BANK : (h + 1) * BANK])
         pick_values(2, b_flat[1][:, : I // 2].bitcast(BF16), True)
         turn_values(1, "bank_b0", buf("val_bf1", [P, Q], F32, on="val_rows2")[:])
+        quantise_values(1)
 
         o_sb = {}
 
@@ -218,28 +226,33 @@ def tile_attend_twopools_written_lean_kernel(
         def place(j):
             nc.scalar.activation(placed[j % 2][:].indirect(row_place[:]), o_sb[j], COPY)
 
-        def finish(j, parts, total):
-            for part in range(parts):
-                cols = slice(part * M // parts, (part + 1) * M // parts)
+        def finish(j, total):
+            for h in range(M // BANK):
+                cols = slice(h * BANK, (h + 1) * BANK)
                 nc.vector.tensor_tensor(total[:, cols], faded[min(j, 1)][:, cols], placed[j % 2][:, cols], ALU.add)
-                nc.sync.dma_start(out[j * P : (j + 1) * P, cols], total[:, cols])
+                if j == blocks - 1:
+                    nc.sync.dma_start(out[j * P : (j + 1) * P, cols], total[:, cols])
+            if j < blocks - 1:
+                nc.sync.dma_start(out[j * P : (j + 1) * P, :], total[:])
 
         turn_values(2, "bank_b1", faded[1][:, 3 * M // 8 : 5 * M // 8])
+        quantise_values(2)
         sum_values(0, "bank_a0", b_flat[1][:, :Q])
         place(0)
         fade_old(0)
         sum_values(1, "bank_b1", buf("o_sb1", [P, Q], F32)[:])
         place(1)
         fade_old(1)
-        pick_values(3, buf("val_picked3", [P, I], BF16, on="old_rows1")[:], False)
-        finish(0, 1, buf("total0", [P, M], F32, on="val_rows3"))
-        sum_values(2, "bank_a1", buf("o_sb2", [P, Q], F32)[:])
-        finish(1, 1, faded[0])
+        pick_values(3, old_rows[1][:, : M // 4].bitcast(BF16), False)
+        finish(0, buf("total0", [P, M], F32, on="val_rows3"))
         turn_values(3, "bank_a0", buf("val_bf3", [P, Q], F32)[:])
+        sum_values(2, "bank_a1", old_rows[1][:, :Q])
+        finish(1, faded[0])
+        quantise_values(3)
         place(2)
         fade_old(2)
         sum_values(3, "bank_b0", buf("o_sb3", [P, Q], F32)[:])
         place(3)
-        finish(2, 1, buf("total2", [P, M], F32))
+        finish(2, old_rows[2])
         fade_old(3)
-        finish(3, 2, faded[1])
+        finish(3, old_rows[3])

@@ -20,6 +20,7 @@ COPY = mybir.ActivationFunctionType.Copy
 P = 128
 PACK = 4
 BANK = 512
+SCALAR_SLOTS = 160
 
 
 def tile_attend_twopools_written_lean_kernel(
@@ -65,13 +66,12 @@ def tile_attend_twopools_written_lean_kernel(
             )
         nc.sync.dma_start(slot_token[:], offs)
         nc.sync.dma_start(key_words[:].bitcast(I32), keys_words[0].bitcast(I32))
-        nc.sync.dma_start(note_planes[1][:], notes_by_plane[1])
+        nc.sync.dma_start(q_raw[0][:], query.rearrange("(p t) q -> p t q", t=PACK))
+        nc.sync.dma_start(q_raw[1][:], query2.rearrange("(p t) q -> p t q", t=PACK))
         nc.sync.dma_start(rows[0:8, :], fade.rearrange("o (r n) -> (o r) n", n=P))
         nc.sync.dma_start(rows[8:10, :], lam.rearrange("(r n) o -> r (n o)", n=P))
-        nc.sync.dma_start(note_planes[2][:], notes_by_plane[2])
-        nc.sync.dma_start(note_planes[3][:], notes_by_plane[3])
-        nc.sync.dma_start(q_raw[1][:], query2.rearrange("(p t) q -> p t q", t=PACK))
-        nc.sync.dma_start(q_raw[0][:], query.rearrange("(p t) q -> p t q", t=PACK))
+        for t in range(1, PACK):
+            nc.sync.dma_start(note_planes[t][:], notes_by_plane[t])
         nc.sync.dma_start(val_rows[0][:], vals[0:P, :])
         nc.sync.dma_start(factor_col[:], slot_factor.rearrange("o (p t) -> p (o t)", t=PACK))
         nc.sync.dma_start(val_rows[1][:], vals[P : 2 * P, :])
@@ -86,23 +86,6 @@ def tile_attend_twopools_written_lean_kernel(
         note_picked = buf("note_picked", [P, PACK, I], BF16)
         key_words_picked = buf("key_words_picked", [P, I], U16)
         key_scales_picked = buf("key_scales_picked", [P, I], U8)
-        nc.vector.tensor_copy(key_words_picked[:], key_words[:].indirect(slot_token[:]))
-        nc.vector.tensor_copy(key_scales_picked[:], key_scales[:].indirect(slot_token[:]))
-        for t in range(PACK - 1):
-            nc.scalar.activation(note_picked[:, t, :], note_planes[t][:].indirect(slot_note[:]), COPY)
-        last = PACK - 1
-        nc.scalar.activation(note_picked[:, last, : I // 2], note_planes[last][:].indirect(slot_note[:, : I // 32]), COPY)
-        nc.vector.tensor_copy(note_picked[:, last, I // 2 :], note_planes[last][:].indirect(slot_note[:, I // 32 :]))
-
-        rows_turned = ps.tile([P, P], F32, name="rows_turned", tag="bank_v0")
-        nc.tensor.transpose(rows_turned[:], rows[:], ident[:])
-        columns = buf("columns", [P, 16], F32, on="note_plane1")
-        nc.scalar.copy(columns[:], rows_turned[:, 0:16])
-        fade_bank = [ps.tile([P, BANK], F32, name="fade_bank%d" % h) for h in range(M // BANK)]
-        for r in range(M // P):
-            h, c = divmod(r, BANK // P)
-            nc.tensor.transpose(fade_bank[h][:, c * P : (c + 1) * P], columns[:, r : r + 1].to_broadcast([P, P]), ident[:])
-
         note_bf = buf("note_bf", [P, I * PACK], BF16)
         note_codes = buf("note_codes", [P, I], U32)
         note_scales = buf("note_scales", [P, I], U8)
@@ -110,30 +93,55 @@ def tile_attend_twopools_written_lean_kernel(
         q_codes = [buf("q_codes%d" % n, [P, Q], U32) for n in range(2)]
         q_scales = [buf("q_scales%d" % n, [P, Q], U8) for n in range(2)]
 
-        nc.vector.tensor_copy(
-            note_bf[:].rearrange("p (c i t) -> p c t i", i=4, t=PACK),
-            note_picked[:].rearrange("p t (c i) -> p c t i", i=4),
-        )
-        for n in (1, 0):
-            nc.scalar.copy(
-                q_bf[n][:].rearrange("p (c i t) -> p c t i", i=4, t=PACK),
-                q_raw[n][:].rearrange("p t (c i) -> p c t i", i=4),
-            )
-        nc.vector.quantize_mx(note_codes[:].bitcast(FP8X4), note_scales[:], note_bf[:])
-        nc.vector.quantize_mx(q_codes[1][:].bitcast(FP8X4), q_scales[1][:], q_bf[1][:])
+        def woven(flat):
+            return flat.rearrange("p (c i t) -> p c t i", i=4, t=PACK)
+
+        def planes(planar):
+            return planar.rearrange("p t (c i) -> p c t i", i=4)
+
+        nc.vector.tensor_copy(key_words_picked[:], key_words[:].indirect(slot_token[:]))
+        nc.vector.tensor_copy(key_scales_picked[:], key_scales[:].indirect(slot_token[:]))
+        nc.scalar.activation(note_picked[:, 0, :], note_planes[0][:].indirect(slot_note[:]), COPY)
+        nc.scalar.copy(woven(q_bf[0][:]), planes(q_raw[0][:]))
         nc.vector.quantize_mx(q_codes[0][:].bitcast(FP8X4), q_scales[0][:], q_bf[0][:])
+        nc.vector.tensor_copy(woven(q_bf[1][:]), planes(q_raw[1][:]))
+        nc.vector.quantize_mx(q_codes[1][:].bitcast(FP8X4), q_scales[1][:], q_bf[1][:])
 
         a_bank = [ps.tile([P, I], F32, name="a_bank%d" % h, tag="bank_a%d" % h) for h in range(halves)]
+        a_flat = [buf("a_flat%d" % h, [P, I], F32) for h in range(halves)]
+        a_sb = [a_flat[h][:].rearrange("q (t s) -> q t s", t=PACK) for h in range(halves)]
+        for h in range(halves):
+            cols = slice(h * P, (h + 1) * P)
+            nc.tensor.matmul_mx(
+                a_bank[h][:], lhsT=q_codes[0][:, cols].bitcast(FP8X4), lhsT_scale=q_scales[0][:, cols],
+                rhs=key_words_picked[:].bitcast(FP4X4), rhs_scale=key_scales_picked[:], start=True, stop=True,
+            )
+            nc.vector.tensor_copy(a_sb[h], a_bank[h][:].rearrange("q (s t) -> q t s", t=PACK))
+
+        rows_turned = ps.tile([P, P], F32, name="rows_turned", tag="bank_v0")
+        nc.tensor.transpose(rows_turned[:], rows[:], ident[:])
+        columns = buf("columns", [P, 16], F32, on="q_raw1")
+        nc.vector.tensor_copy(columns[:], rows_turned[:, 0:16])
+        fade_bank = [ps.tile([P, BANK], F32, name="fade_bank%d" % h) for h in range(M // BANK)]
+        for r in range(M // P):
+            h, c = divmod(r, BANK // P)
+            nc.tensor.transpose(fade_bank[h][:, c * P : (c + 1) * P], columns[:, r : r + 1].to_broadcast([P, P]), ident[:])
+
+        for t in range(1, PACK - 1):
+            nc.scalar.activation(note_picked[:, t, :], note_planes[t][:].indirect(slot_note[:]), COPY)
+        last = PACK - 1
+        nc.scalar.activation(note_picked[:, last, : I // 2], note_planes[last][:].indirect(slot_note[:, : I // 32]), COPY)
+        nc.vector.tensor_copy(note_picked[:, last, I // 2 :], note_planes[last][:].indirect(slot_note[:, I // 32 :]))
+        nc.scalar.copy(woven(note_bf[:, : PACK * SCALAR_SLOTS]), planes(note_picked[:, :, :SCALAR_SLOTS]))
+        nc.vector.tensor_copy(woven(note_bf[:, PACK * SCALAR_SLOTS :]), planes(note_picked[:, :, SCALAR_SLOTS:]))
+        nc.vector.quantize_mx(note_codes[:].bitcast(FP8X4), note_scales[:], note_bf[:])
+
         b_bank = [ps.tile([P, I], F32, name="b_bank%d" % h, tag="bank_b%d" % h) for h in range(halves)]
         for h in range(halves):
             cols = slice(h * P, (h + 1) * P)
             nc.tensor.matmul_mx(
                 b_bank[h][:], lhsT=q_codes[1][:, cols].bitcast(FP8X4), lhsT_scale=q_scales[1][:, cols],
                 rhs=note_codes[:].bitcast(FP8X4), rhs_scale=note_scales[:], start=True, stop=True,
-            )
-            nc.tensor.matmul_mx(
-                a_bank[h][:], lhsT=q_codes[0][:, cols].bitcast(FP8X4), lhsT_scale=q_scales[0][:, cols],
-                rhs=key_words_picked[:].bitcast(FP4X4), rhs_scale=key_scales_picked[:], start=True, stop=True,
             )
 
         val_codes = [buf("val_codes%d" % j, [P, P], U32) for j in range(blocks)]
@@ -165,24 +173,20 @@ def tile_attend_twopools_written_lean_kernel(
 
         faded = [buf("faded%d" % n, [P, M], F32) for n in range(2)]
         w_bf = faded[0][:, M // 4 : 3 * M // 4].bitcast(BF16)
-        b_flat = [buf("b_flat%d" % h, [P, I], F32) for h in range(halves)]
-        b_sb = [b_flat[h][:].rearrange("q (t s) -> q t s", t=PACK) for h in range(halves)]
         larger = [buf("larger%d" % h, [P, PACK, P], F32) for h in range(halves)]
         smaller_flat = [buf("smaller_flat%d" % h, [P, I], F32) for h in range(halves)]
         smaller = [smaller_flat[h][:].rearrange("q (t s) -> q t s", t=PACK) for h in range(halves)]
         smaller_lam = [buf("smaller_lam%d" % h, [P, PACK, P], F32) for h in range(halves)]
-        a_dealt = [a_bank[h][:].rearrange("q (s t) -> q t s", t=PACK) for h in range(halves)]
-        pick_values(0, buf("val_picked0", [P, I], BF16, on="q_raw0")[:], True)
+        b_dealt = [b_bank[h][:].rearrange("q (s t) -> q t s", t=PACK) for h in range(halves)]
+        pick_values(0, buf("val_picked0", [P, I], BF16)[:], True)
         for h in range(halves):
-            nc.scalar.copy(b_sb[h], b_bank[h][:].rearrange("q (s t) -> q t s", t=PACK))
-        turn_values(0, "bank_v0", faded[0][:, M // 2 : 3 * M // 4])
-        quantise_values(0)
-        for h in range(halves):
-            nc.vector.tensor_tensor(smaller[h], a_dealt[h], b_sb[h], ALU.min)
+            nc.vector.tensor_tensor(smaller[h], b_dealt[h], a_sb[h], ALU.min)
             nc.scalar.activation(smaller_lam[h][:], smaller[h], COPY, scale=columns[:, 8 + h : 9 + h])
+        turn_values(0, "bank_v0", faded[0][:, M // 2 : 3 * M // 4])
         for h in range(halves):
-            nc.vector.tensor_tensor(larger[h][:], a_dealt[h], b_sb[h], ALU.max)
-        s_bank = [ps.tile([P, PACK, P], F32, name="s_bank%d" % h, tag="bank_b%d" % h) for h in range(halves)]
+            nc.vector.tensor_tensor(larger[h][:], b_dealt[h], a_sb[h], ALU.max)
+        quantise_values(0)
+        s_bank = [ps.tile([P, PACK, P], F32, name="s_bank%d" % h, tag="bank_a%d" % h) for h in range(halves)]
         for h in range(halves):
             for t in range(PACK):
                 nc.tensor.matmul(s_bank[h][:, t, :], smaller_lam[h][:, t, :], ident[:], start=(t == 0), stop=False, is_transpose=True)
@@ -203,8 +207,8 @@ def tile_attend_twopools_written_lean_kernel(
         for h in range(halves):
             cols = slice(h * P, (h + 1) * P)
             nc.vector.quantize_mx(w_codes[:, cols].bitcast(FP8X4), w_scales[:, cols], w_bf[:, h * BANK : (h + 1) * BANK])
-        pick_values(2, b_flat[1][:, : I // 2].bitcast(BF16), True)
-        turn_values(1, "bank_b0", buf("val_bf1", [P, Q], F32, on="val_rows2")[:])
+        pick_values(2, a_flat[1][:, : I // 2].bitcast(BF16), True)
+        turn_values(1, "bank_a0", buf("val_bf1", [P, Q], F32, on="val_rows2")[:])
         quantise_values(1)
 
         o_sb = {}
@@ -235,23 +239,23 @@ def tile_attend_twopools_written_lean_kernel(
             if j < blocks - 1:
                 nc.sync.dma_start(out[j * P : (j + 1) * P, :], total[:])
 
-        turn_values(2, "bank_b1", faded[1][:, 3 * M // 8 : 5 * M // 8])
+        turn_values(2, "bank_a1", faded[1][:, 3 * M // 8 : 5 * M // 8])
         quantise_values(2)
-        sum_values(0, "bank_a0", b_flat[1][:, :Q])
+        sum_values(0, "bank_b0", a_flat[1][:, :Q])
         place(0)
         fade_old(0)
-        sum_values(1, "bank_b1", buf("o_sb1", [P, Q], F32)[:])
+        sum_values(1, "bank_a1", buf("o_sb1", [P, Q], F32)[:])
         place(1)
         fade_old(1)
         pick_values(3, old_rows[1][:, : M // 4].bitcast(BF16), False)
         finish(0, buf("total0", [P, M], F32, on="val_rows3"))
-        turn_values(3, "bank_a0", buf("val_bf3", [P, Q], F32)[:])
-        sum_values(2, "bank_a1", old_rows[1][:, :Q])
+        turn_values(3, "bank_b0", buf("val_bf3", [P, Q], F32)[:])
+        sum_values(2, "bank_b1", old_rows[1][:, :Q])
         finish(1, faded[0])
         quantise_values(3)
         place(2)
         fade_old(2)
-        sum_values(3, "bank_b0", buf("o_sb3", [P, Q], F32)[:])
+        sum_values(3, "bank_a0", buf("o_sb3", [P, Q], F32)[:])
         place(3)
         finish(2, old_rows[2])
         fade_old(3)

from contextlib import ExitStack

import concourse.mybir as mybir
from concourse.masks import make_identity

D, T, I, Q, E, U, M = 512, 2048, 512, 256, 512, 1024, 1024
FLOPS = 2 * Q * I * D * 2 + 2 * E * Q * I

F32 = mybir.dt.float32
BF16 = mybir.dt.bfloat16
I32 = mybir.dt.int32
U32 = mybir.dt.uint32
U16 = mybir.dt.uint16
U8 = mybir.dt.uint8
FP8X4 = mybir.dt.float8_e4m3fn_x4
FP4X4 = mybir.dt.float4_e2m1fn_x4
ALU = mybir.AluOpType
COPY = mybir.ActivationFunctionType.Copy

P = 128
PACK = 4
BANK = 512
SCALAR_SLOTS = 160


def tile_attend_twopools_written_lean_kernel(
    tc, query, keys_words, keys_scales, query2, notes, lam, slot_factor, vals, old, fade, offs, offs2, offs3, out
):
    nc = tc.nc
    halves = Q // P
    blocks = E // P
    with ExitStack() as ctx:
        sb = ctx.enter_context(tc.tile_pool(name="sb", bufs=1))
        ps = ctx.enter_context(tc.psum_pool(name="ps", bufs=1))

        def buf(name, shape, dtype, on=None):
            return sb.tile(shape, dtype, name=name, tag=on or name, align_bytes=64)

        slot_token = buf("slot_token", [P, I // 16], U16)
        slot_note = buf("slot_note", [P, I // 16], U16)
        row_place = buf("row_place", [P, Q // 16], U16)
        key_words = buf("key_words", [P, T], U16)
        key_scales = buf("key_scales", [P, T], U8)
        note_planes = [buf("note_plane%d" % t, [P, U], F32) for t in range(PACK)]
        q_raw = [buf("q_raw%d" % n, [P, PACK, Q], F32) for n in range(2)]
        val_rows = [buf("val_rows%d" % j, [P, T], F32) for j in range(blocks)]
        old_rows = [buf("old_rows%d" % j, [P, M], F32) for j in range(blocks)]
        placed = [buf("placed%d" % j, [P, M], F32) for j in range(2)]
        rows = buf("rows", [P, P], F32)
        factor_col = buf("factor_col", [P, PACK], F32)
        ident = buf("ident", [P, P], F32)

        nc.vector.memset(key_scales[:].bitcast(I32), 0)
        nc.vector.memset(rows[:], 0.0)
        for w in placed:
            nc.vector.memset(w[:], 0.0)
        make_identity(nc, ident[:])

        notes_by_plane = notes.rearrange("(p t) u -> t p u", t=PACK)
        nc.sync.dma_start(slot_note[:], offs2)
        nc.sync.dma_start(note_planes[0][:], notes_by_plane[0])
        for quad in range(4):
            nc.sync.dma_start(
                key_scales[32 * quad : 32 * quad + 4, :].bitcast(I32),
                keys_scales[0, 4 * quad : 4 * quad + 4, :].bitcast(I32),
            )
        nc.sync.dma_start(slot_token[:], offs)
        nc.sync.dma_start(key_words[:].bitcast(I32), keys_words[0].bitcast(I32))
        nc.sync.dma_start(q_raw[0][:], query.rearrange("(p t) q -> p t q", t=PACK))
        nc.sync.dma_start(q_raw[1][:], query2.rearrange("(p t) q -> p t q", t=PACK))
        nc.sync.dma_start(rows[0:8, :], fade.rearrange("o (r n) -> (o r) n", n=P))
        nc.sync.dma_start(rows[8:10, :], lam.rearrange("(r n) o -> r (n o)", n=P))
        for t in range(1, PACK):
            nc.sync.dma_start(note_planes[t][:], notes_by_plane[t])
        nc.sync.dma_start(val_rows[0][:], vals[0:P, :])
        nc.sync.dma_start(factor_col[:], slot_factor.rearrange("o (p t) -> p (o t)", t=PACK))
        nc.sync.dma_start(val_rows[1][:], vals[P : 2 * P, :])
        nc.sync.dma_start(row_place[:], offs3)
        nc.sync.dma_start(val_rows[2][:], vals[2 * P : 3 * P, :])
        nc.sync.dma_start(old_rows[0][:], old[0:P, :])
        nc.sync.dma_start(old_rows[1][:], old[P : 2 * P, :])
        nc.sync.dma_start(val_rows[3][:], vals[3 * P : 4 * P, :])
        nc.sync.dma_start(old_rows[2][:], old[2 * P : 3 * P, :])
        nc.sync.dma_start(old_rows[3][:], old[3 * P : 4 * P, :])

        note_picked = buf("note_picked", [P, PACK, I], BF16)
        key_words_picked = buf("key_words_picked", [P, I], U16)
        key_scales_picked = buf("key_scales_picked", [P, I], U8)
        note_bf = buf("note_bf", [P, I * PACK], BF16)
        note_codes = buf("note_codes", [P, I], U32)
        note_scales = buf("note_scales", [P, I], U8)
        q_bf = [buf("q_bf%d" % n, [P, Q * PACK], BF16) for n in range(2)]
        q_codes = [buf("q_codes%d" % n, [P, Q], U32) for n in range(2)]
        q_scales = [buf("q_scales%d" % n, [P, Q], U8) for n in range(2)]

        def woven(flat):
            return flat.rearrange("p (c i t) -> p c t i", i=4, t=PACK)

        def planes(planar):
            return planar.rearrange("p t (c i) -> p c t i", i=4)

        nc.vector.tensor_copy(key_words_picked[:], key_words[:].indirect(slot_token[:]))
        nc.vector.tensor_copy(key_scales_picked[:], key_scales[:].indirect(slot_token[:]))
        nc.scalar.activation(note_picked[:, 0, :], note_planes[0][:].indirect(slot_note[:]), COPY)
        nc.scalar.copy(woven(q_bf[0][:]), planes(q_raw[0][:]))
        nc.vector.quantize_mx(q_codes[0][:].bitcast(FP8X4), q_scales[0][:], q_bf[0][:])
        nc.vector.tensor_copy(woven(q_bf[1][:]), planes(q_raw[1][:]))
        nc.vector.quantize_mx(q_codes[1][:].bitcast(FP8X4), q_scales[1][:], q_bf[1][:])

        a_bank = [ps.tile([P, I], F32, name="a_bank%d" % h, tag="bank_a%d" % h) for h in range(halves)]
        a_flat = [buf("a_flat%d" % h, [P, I], F32) for h in range(halves)]
        a_sb = [a_flat[h][:].rearrange("q (t s) -> q t s", t=PACK) for h in range(halves)]
        for h in range(halves):
            cols = slice(h * P, (h + 1) * P)
            nc.tensor.matmul_mx(
                a_bank[h][:], lhsT=q_codes[0][:, cols].bitcast(FP8X4), lhsT_scale=q_scales[0][:, cols],
                rhs=key_words_picked[:].bitcast(FP4X4), rhs_scale=key_scales_picked[:], start=True, stop=True,
            )
            nc.vector.tensor_copy(a_sb[h], a_bank[h][:].rearrange("q (s t) -> q t s", t=PACK))

        rows_turned = ps.tile([P, P], F32, name="rows_turned", tag="bank_v0")
        nc.tensor.transpose(rows_turned[:], rows[:], ident[:])
        columns = buf("columns", [P, 16], F32, on="q_raw1")
        nc.vector.tensor_copy(columns[:], rows_turned[:, 0:16])
        fade_bank = [ps.tile([P, BANK], F32, name="fade_bank%d" % h) for h in range(M // BANK)]
        for r in range(M // P):
            h, c = divmod(r, BANK // P)
            nc.tensor.transpose(fade_bank[h][:, c * P : (c + 1) * P], columns[:, r : r + 1].to_broadcast([P, P]), ident[:])

        for t in range(1, PACK - 1):
            nc.scalar.activation(note_picked[:, t, :], note_planes[t][:].indirect(slot_note[:]), COPY)
        last = PACK - 1
        nc.scalar.activation(note_picked[:, last, : I // 2], note_planes[last][:].indirect(slot_note[:, : I // 32]), COPY)
        nc.vector.tensor_copy(note_picked[:, last, I // 2 :], note_planes[last][:].indirect(slot_note[:, I // 32 :]))
        nc.scalar.copy(woven(note_bf[:, : PACK * SCALAR_SLOTS]), planes(note_picked[:, :, :SCALAR_SLOTS]))
        nc.vector.tensor_copy(woven(note_bf[:, PACK * SCALAR_SLOTS :]), planes(note_picked[:, :, SCALAR_SLOTS:]))
        nc.vector.quantize_mx(note_codes[:].bitcast(FP8X4), note_scales[:], note_bf[:])

        b_bank = [ps.tile([P, I], F32, name="b_bank%d" % h, tag="bank_b%d" % h) for h in range(halves)]
        for h in range(halves):
            cols = slice(h * P, (h + 1) * P)
            nc.tensor.matmul_mx(
                b_bank[h][:], lhsT=q_codes[1][:, cols].bitcast(FP8X4), lhsT_scale=q_scales[1][:, cols],
                rhs=note_codes[:].bitcast(FP8X4), rhs_scale=note_scales[:], start=True, stop=True,
            )

        val_codes = [buf("val_codes%d" % j, [P, P], U32) for j in range(blocks)]
        val_scales = [buf("val_scales%d" % j, [P, P], U8) for j in range(blocks)]
        val_picked = {}
        val_words = {}

        def pick_values(j, into, by_scalar):
            val_picked[j] = into
            window = val_rows[j][:].indirect(slot_token[:])
            if by_scalar:
                nc.scalar.activation(into, window, COPY)
            else:
                nc.vector.tensor_copy(into, window)

        def turn_values(j, bank, val_bf):
            words = val_picked[j].bitcast(F32)
            turned = ps.tile([P, 2, P], F32, name="val_turned%d" % j, tag=bank)
            for u in range(2):
                nc.tensor.transpose(turned[:, u, :], words[:, u : I // 2 : 2], ident[:])
            nc.scalar.copy(
                val_bf.rearrange("p (e u) -> p e u", u=2),
                turned[:].rearrange("p u e -> p e u"),
            )
            val_words[j] = val_bf

        def quantise_values(j):
            nc.vector.quantize_mx(val_codes[j][:].bitcast(FP8X4), val_scales[j][:], val_words[j].bitcast(BF16))

        faded = [buf("faded%d" % n, [P, M], F32) for n in range(2)]
        w_bf = faded[0][:, M // 4 : 3 * M // 4].bitcast(BF16)
        larger = [buf("larger%d" % h, [P, PACK, P], F32) for h in range(halves)]
        smaller_flat = [buf("smaller_flat%d" % h, [P, I], F32) for h in range(halves)]
        smaller = [smaller_flat[h][:].rearrange("q (t s) -> q t s", t=PACK) for h in range(halves)]
        smaller_lam = [buf("smaller_lam%d" % h, [P, PACK, P], F32) for h in range(halves)]
        b_dealt = [b_bank[h][:].rearrange("q (s t) -> q t s", t=PACK) for h in range(halves)]
        pick_values(0, buf("val_picked0", [P, I], BF16)[:], True)
        for h in range(halves):
            nc.vector.tensor_tensor(smaller[h], b_dealt[h], a_sb[h], ALU.min)
            nc.scalar.activation(smaller_lam[h][:], smaller[h], COPY, scale=columns[:, 8 + h : 9 + h])
        turn_values(0, "bank_v0", faded[0][:, M // 2 : 3 * M // 4])
        for h in range(halves):
            nc.vector.tensor_tensor(larger[h][:], b_dealt[h], a_sb[h], ALU.max)
        quantise_values(0)
        s_bank = [ps.tile([P, PACK, P], F32, name="s_bank%d" % h, tag="bank_a%d" % h) for h in range(halves)]
        for h in range(halves):
            for t in range(PACK):
                nc.tensor.matmul(s_bank[h][:, t, :], smaller_lam[h][:, t, :], ident[:], start=(t == 0), stop=False, is_transpose=True)
            for t in range(PACK):
                nc.tensor.matmul(s_bank[h][:, t, :], larger[h][:, t, :], ident[:], start=False, stop=(t == PACK - 1), is_transpose=True)
        pick_values(1, smaller_flat[0][:, : I // 2].bitcast(BF16), True)
        for h in range(halves):
            nc.vector.scalar_tensor_tensor(
                w_bf[:, h * BANK : (h + 1) * BANK].rearrange("p (q t) -> p q t", t=PACK),
                s_bank[h][:].rearrange("p t q -> p q t"),
                0.0,
                factor_col[:].unsqueeze(1).to_broadcast([P, P, PACK]),
                ALU.max,
                ALU.mult,
            )
        w_codes = buf("w_codes", [P, Q], U32)
        w_scales = buf("w_scales", [P, Q], U8)
        for h in range(halves):
            cols = slice(h * P, (h + 1) * P)
            nc.vector.quantize_mx(w_codes[:, cols].bitcast(FP8X4), w_scales[:, cols], w_bf[:, h * BANK : (h + 1) * BANK])
        pick_values(2, a_flat[1][:, : I // 2].bitcast(BF16), True)
        turn_values(1, "bank_a0", buf("val_bf1", [P, Q], F32, on="val_rows2")[:])
        quantise_values(1)

        o_sb = {}

        def fade_old(j):
            for h in range(M // BANK):
                cols = slice(h * BANK, (h + 1) * BANK)
                nc.vector.tensor_tensor(faded[min(j, 1)][:, cols], old_rows[j][:, cols], fade_bank[h][:], ALU.mult)

        def sum_values(j, bank, into):
            o_bank = ps.tile([P, Q], F32, name="o_bank%d" % j, tag=bank)
            nc.tensor.matmul_mx(
                o_bank[:], lhsT=val_codes[j][:].bitcast(FP8X4), lhsT_scale=val_scales[j][:],
                rhs=w_codes[:].bitcast(FP8X4), rhs_scale=w_scales[:], start=True, stop=True,
            )
            o_sb[j] = into
            nc.scalar.copy(into, o_bank[:])

        def place(j):
            nc.scalar.activation(placed[j % 2][:].indirect(row_place[:]), o_sb[j], COPY)

        def finish(j, total):
            for h in range(M // BANK):
                cols = slice(h * BANK, (h + 1) * BANK)
                nc.vector.tensor_tensor(total[:, cols], faded[min(j, 1)][:, cols], placed[j % 2][:, cols], ALU.add)
                if j == blocks - 1:
                    nc.sync.dma_start(out[j * P : (j + 1) * P, cols], total[:, cols])
            if j < blocks - 1:
                nc.sync.dma_start(out[j * P : (j + 1) * P, :], total[:])

        turn_values(2, "bank_a1", faded[1][:, 3 * M // 8 : 5 * M // 8])
        quantise_values(2)
        sum_values(0, "bank_b0", a_flat[1][:, :Q])
        place(0)
        fade_old(0)
        sum_values(1, "bank_a1", buf("o_sb1", [P, Q], F32)[:])
        place(1)
        fade_old(1)
        pick_values(3, old_rows[1][:, : M // 4].bitcast(BF16), False)
        finish(0, buf("total0", [P, M], F32, on="val_rows3"))
        turn_values(3, "bank_b0", buf("val_bf3", [P, Q], F32)[:])
        sum_values(2, "bank_b1", old_rows[1][:, :Q])
        finish(1, faded[0])
        quantise_values(3)
        place(2)
        fade_old(2)
        sum_values(3, "bank_a0", buf("o_sb3", [P, Q], F32)[:])
        place(3)
        finish(2, old_rows[2])
        fade_old(3)
        finish(3, old_rows[3])
